import numpy as np
import ml_dtypes


def mxq(x, axis, fmt="e4m3"):
    dtype, down = {"e4m3": (ml_dtypes.float8_e4m3fn, 7), "e5m2": (ml_dtypes.float8_e5m2, 14)}[fmt]
    v = np.moveaxis(np.asarray(x, np.float32).astype(ml_dtypes.bfloat16).astype(np.float64), axis, -1)
    blocks = v.reshape(v.shape[:-1] + (-1, 32))
    amax = np.abs(blocks).max(-1, keepdims=True)
    byte = np.maximum(np.where(amax > 0, np.frexp(amax)[1] - 1 + 127, 0) - down, 1)
    scale = np.exp2(byte - 127.0)
    codes = (blocks / scale).astype(np.float32).astype(dtype).astype(np.float64)
    return np.moveaxis((codes * scale).reshape(v.shape), -1, axis)


WIDE = False


def mx_kscale(k):
    if not WIDE:
        return np.ones(k)
    levels = np.array([10, -10, 5, -5, 0])
    if k % 512:
        return np.exp2(np.random.permutation(np.resize(levels, k // 32))).repeat(32)
    a = np.empty((k // 512, 16))
    for p in range(k // 512):
        a[p, :8] = np.random.permutation(np.resize(levels, 8))
        for g in range(8):
            far = levels[np.abs(levels - a[p, g]) >= 10]
            a[p, g + 8] = far[np.random.randint(len(far))]
    return np.exp2(a.ravel()).repeat(32)


def f64(x):
    return np.asarray(x).astype(np.float64)


def striped(idx):
    return np.tile(idx.reshape(-1, 16).T, (8, 1)).astype(np.uint16)


def unstriped(offs):
    return offs[:16].T.reshape(-1).astype(np.int64)


def pack_weight(w):
    k, n = w.shape
    w = f64(np.asarray(w, np.float32).astype(ml_dtypes.bfloat16)).reshape(k // 32, 32, n)
    amax = np.abs(w).max(1)
    byte = np.clip(np.where(amax > 0, np.frexp(amax)[1] - 1 + 127 - 7, 1), 1, 254)
    scaled = (w * np.exp2(127.0 - byte)[:, None, :]).reshape(k, n).astype(np.float32)
    words = np.ascontiguousarray(scaled.reshape(k // 512, 128, 4, n).transpose(0, 1, 3, 2)).astype(ml_dtypes.float8_e4m3fn).view(np.uint8)
    return words, np.ascontiguousarray(byte.astype(np.uint8).reshape(k // 512, 16, n))


def unpack_weight(words, scales):
    g, p, n, _ = words.shape
    vals = np.ascontiguousarray(words).view(ml_dtypes.float8_e4m3fn).astype(np.float64) * np.repeat(np.exp2(scales.astype(np.float64) - 127.0), 8, axis=1)[..., None]
    return vals.transpose(0, 1, 3, 2).reshape(g * 512, n)


E2M1 = np.array([0.0, 0.5, 1.0, 1.5, 2.0, 3.0, 4.0, 6.0, -0.0, -0.5, -1.0, -1.5, -2.0, -3.0, -4.0, -6.0])


def pack_fp4(w):
    k, n = w.shape
    w = f64(np.asarray(w, np.float32).astype(ml_dtypes.bfloat16)).reshape(k // 32, 32, n)
    amax = np.abs(w).max(1)
    mant, ex = np.frexp(amax / 6.0)
    byte = np.clip(np.where(amax > 0, np.where(mant > 0.5, ex, ex - 1) + 127, 1), 1, 254)
    scaled = (w * np.exp2(127.0 - byte)[:, None, :]).reshape(k, n).astype(np.float32)
    c = np.ascontiguousarray(scaled.reshape(k // 512, 128, 4, n).transpose(0, 1, 3, 2)).astype(ml_dtypes.float4_e2m1fn).view(np.uint8) & 0xF
    words = (c[..., 0::2] | (c[..., 1::2] << 4)).reshape(k // 512, 128, 2 * n)
    return np.ascontiguousarray(words), np.ascontiguousarray(byte.astype(np.uint8).reshape(k // 512, 16, n))


def unpack_fp4(words, scales):
    g, _, n = scales.shape
    words = np.ascontiguousarray(words).reshape(g, 128, n, 2)
    nib = np.empty((g, 128, n, 4), np.uint8)
    nib[..., 0::2] = words & 0xF
    nib[..., 1::2] = words >> 4
    vals = E2M1[nib] * np.repeat(np.exp2(scales.astype(np.float64) - 127.0), 8, axis=1)[..., None]
    return vals.transpose(0, 1, 3, 2).reshape(g * 512, n)


def relu(v):
    return np.maximum(v, 0.0)


K, T, S, D, N, H = 512, 2048, 1024, 4, 128, 512


def setup_inputs():
    n = np.random.standard_normal
    s = mx_kscale(K)[:, None]
    u = mx_kscale(H)
    packed_xT = pack_weight(n((K, T)) * s)
    packed_w1 = pack_fp4(n((K, H)) / np.sqrt(K) / s)
    packed_w2 = pack_fp4(n((K, H)) / np.sqrt(K) / s)
    packed_w3 = pack_fp4(n((H, N)) / np.sqrt(H) / u[:, None])
    return {
        "x_words": packed_xT[0],
        "x_scales": packed_xT[1],
        "w1_words": packed_w1[0],
        "w1_scales": packed_w1[1],
        "w2_words": packed_w2[0],
        "w2_scales": packed_w2[1],
        "ctf": (np.random.uniform(-1.0, 1.0, (H, S))).astype(np.float32),
        "unit": (np.random.uniform(0.6, 1.4, (H, 1)) * u[:, None]).astype(np.float32),
        "w3_words": packed_w3[0],
        "w3_scales": packed_w3[1],
        "offs": striped(np.random.permutation(T)[:S]),
        "half": striped(np.random.permutation(S)),
    }


def reference(x_words, x_scales, w1_words, w1_scales, w2_words, w2_scales, ctf, unit, w3_words, w3_scales, offs, half):
    xq = unpack_weight(x_words, x_scales)[:, unstriped(offs)]
    re = unpack_fp4(w1_words, w1_scales).T @ xq
    ra = f64(ctf) * re
    ah = re[:, unstriped(half)]
    rb = f64(ctf) * ah
    xc = ra * rb
    num = xc.reshape(len(xc), -1, D).sum(axis=2)
    pa = (ra) ** 2
    ea = pa.reshape(len(pa), -1, D).sum(axis=2) + 0.3
    pb = (rb) ** 2
    eb = pb.reshape(len(pb), -1, D).sum(axis=2) + 0.3
    fsc = num / np.sqrt(ea * eb)
    wien = relu(fsc + 0.6) / (np.abs(fsc) + 0.5)
    im2 = unpack_fp4(w2_words, w2_scales).T @ xq
    filt = np.repeat(wien, D, axis=1) * ra - (0.4 * im2)
    hid = f64(unit) * (filt * f64(ctf) + rb)
    return unpack_fp4(w3_words, w3_scales).T @ mxq(hid, 0, "e4m3")

@@ -1,0 +1,242 @@
+from contextlib import ExitStack
+
+import concourse.mybir as mybir
+from concourse.masks import make_identity
+
+K, T, S, D, N, H = 512, 2048, 1024, 4, 128, 512
+FLOPS = 2 * K * H * S * 2 + 2 * H * N * S
+
+F32 = mybir.dt.float32
+BF16 = mybir.dt.bfloat16
+I32 = mybir.dt.int32
+U32 = mybir.dt.uint32
+U16 = mybir.dt.uint16
+U8 = mybir.dt.uint8
+FP8X4 = mybir.dt.float8_e4m3fn_x4
+FP4X4 = mybir.dt.float4_e2m1fn_x4
+ACT = mybir.ActivationFunctionType
+ALU = mybir.AluOpType
+
+P = 128
+PACK = 4
+BANK = 512
+LIST_ROWS = 16
+CHUNKS = (128, 128, 256, 256, 128, 128)
+VECTOR_GATHERS = (1,)
+
+
+def tile_picked_ycryoem_ctf_p_kernel(
+    tc, x_words, x_scales, w1_words, w1_scales, w2_words, w2_scales, ctf, unit, w3_words, w3_scales, offs, half, out
+):
+    nc = tc.nc
+    with ExitStack() as ctx:
+        lists = ctx.enter_context(tc.tile_pool(name="lists", bufs=1))
+        keep = ctx.enter_context(tc.tile_pool(name="keep", bufs=1))
+        ring = ctx.enter_context(tc.tile_pool(name="ring", bufs=3))
+        psum = ctx.enter_context(tc.psum_pool(name="psum", bufs=1))
+
+        def bank(tag, bufs):
+            return psum.tile([P, BANK], F32, name=tag, tag=tag, bufs=bufs)
+
+        def load_scale_rows(queue, plane, scales):
+            for q in range(4):
+                queue.dma_start(plane[32 * q : 32 * q + 4, :].bitcast(I32), scales[0, 4 * q : 4 * q + 4, :].bitcast(I32))
+
+        def deal(engine, dealt, raw, width):
+            run = 16 // width
+            engine.tensor_copy(
+                dealt.rearrange("p (t c i b) -> p c t i b", t=PACK, i=run, b=width),
+                raw.rearrange("p (c i t b) -> p c t i b", t=PACK, i=run, b=width),
+            )
+
+        offs_sb = lists.tile([P, S // LIST_ROWS], U16)
+        half_sb = lists.tile([P, S // LIST_ROWS], U16)
+        xw = keep.tile([P, T], I32, tag="first", bufs=1, align_bytes=64)
+        xs = keep.tile([P, T], U8, tag="second", bufs=1)
+        w1_raw = keep.tile([P, 2 * H], U8, tag="third", bufs=1)
+        ws_raw = keep.tile([P, H], U8, align_bytes=64)
+        u_sb = keep.tile([P, PACK], F32)
+        ident = keep.tile([P, P], F32)
+
+        nc.gpsimd.memset(xs[:].bitcast(I32), 0)
+        nc.gpsimd.memset(ws_raw[:].bitcast(I32), 0)
+        nc.sync.dma_start(offs_sb[:], offs)
+        nc.sync.dma_start(w1_raw[:].bitcast(I32), w1_words[0].bitcast(I32))
+        nc.sync.dma_start(xw[:], x_words[0].rearrange("p n t -> p (n t)").bitcast(I32))
+        nc.sync.dma_start(half_sb[:], half)
+        load_scale_rows(nc.scalar, xs, x_scales)
+        load_scale_rows(nc.gpsimd, ws_raw, w1_scales)
+        nc.gpsimd.dma_start(u_sb[:], unit.rearrange("(p t) o -> p (t o)", t=PACK))
+        make_identity(nc, ident[:])
+
+        w1w = keep.tile([P, 2 * H], U8, align_bytes=64)
+        w1s = keep.tile([P, H], U8, align_bytes=64)
+        w2w = keep.tile([P, 2 * H], U8, align_bytes=64)
+        w2s = keep.tile([P, H], U8, align_bytes=64)
+        deal(nc.vector, w1w[:], w1_raw[:], 2)
+        deal(nc.vector, w1s[:], ws_raw[:], 1)
+
+        c_sb = keep.tile([P, PACK, S], F32, tag="third", bufs=1)
+        ctf_rows = ctf.rearrange("(p t) j -> p t j", t=PACK)
+        for h in range(S // BANK):
+            for t0 in range(0, PACK, 2):
+                cols = slice(h * BANK, (h + 1) * BANK)
+                nc.sync.dma_start(c_sb[:, t0 : t0 + 2, cols], ctf_rows[:, t0 : t0 + 2, cols])
+        load_scale_rows(nc.sync, ws_raw, w2_scales)
+        deal(nc.gpsimd, w2s[:], ws_raw[:], 1)
+
+        gw = keep.tile([P, S], U32, align_bytes=64)
+        gs = keep.tile([P, S], U8, align_bytes=64)
+
+        def product(dst, words, scales, t, cols):
+            nc.tensor.matmul_mx(
+                out=dst,
+                lhsT=words[:, 2 * P * t : 2 * P * (t + 1)].bitcast(FP4X4),
+                lhsT_scale=scales[:, P * t : P * (t + 1)],
+                rhs=gw[:, cols].bitcast(FP8X4),
+                rhs_scale=gs[:, cols],
+                start=True,
+                stop=True,
+            )
+
+        halves = S // BANK
+        nc.vector.tensor_copy(gs[:], xs[:].indirect(offs_sb[:]))
+        re_sb = [keep.tile([P, S], F32, name="re%d" % t) for t in range(PACK)]
+        ra_sb = [keep.tile([P, BANK // P, PACK, P], F32, name="ra%d" % h) for h in range(halves)]
+        re_banks = [("im", 3), ("im", 3), ("im", 3), ("o", 1), ("sab", 2), ("sab", 2), ("nw", 2), ("nw", 2)]
+        for h in range(halves):
+            cols = slice(h * BANK, (h + 1) * BANK)
+            picks = offs_sb[:, h * BANK // LIST_ROWS : (h + 1) * BANK // LIST_ROWS]
+            nc.vector.tensor_copy(gw[:, cols], xw[:].bitcast(U32).indirect(picks))
+        for h in range(halves):
+            cols = slice(h * BANK, (h + 1) * BANK)
+            for t in range(PACK):
+                re_ps = bank(*re_banks[PACK * h + t])
+                product(re_ps[:], w1w, w1s, t, cols)
+                nc.scalar.copy(re_sb[t][:, cols], re_ps[:])
+                nc.vector.tensor_tensor(
+                    ra_sb[h][:, :, t, :],
+                    re_ps[:].rearrange("p (b j) -> p b j", j=P),
+                    c_sb[:, t, cols].rearrange("p (b j) -> p b j", j=P),
+                    ALU.mult,
+                )
+
+        w2_raw = keep.tile([P, 2 * H], U8, tag="second", bufs=1)
+        nc.sync.dma_start(w2_raw[:].bitcast(I32), w2_words[0].bitcast(I32))
+        deal(nc.gpsimd, w2w[:], w2_raw[:], 2)
+        w3w = keep.tile([P, 2 * N], U8, tag="first", bufs=1, align_bytes=64)
+        nc.sync.dma_start(w3w[:].bitcast(I32), w3_words[0].bitcast(I32))
+        w3s = ws_raw[:, 0:N]
+        load_scale_rows(nc.sync, w3s, w3_scales)
+        cu = keep.tile([P, PACK, S], F32)
+        for h in range(halves):
+            cols = slice(h * BANK, (h + 1) * BANK)
+            for t in range(PACK):
+                nc.gpsimd.tensor_scalar(cu[:, t, cols], c_sb[:, t, cols], u_sb[:, t : t + 1], 0.0, ALU.mult, ALU.add)
+
+        j0 = 0
+        for n, w in enumerate(CHUNKS):
+            cols = slice(j0, j0 + w)
+            nb = w // P
+            b0 = (j0 % BANK) // P
+            ra = ra_sb[j0 // BANK][:, b0 : b0 + nb, :, :].rearrange("p b t j -> p (b t j)")
+            ah = ring.tile([P, PACK, w], F32)
+            for t in range(PACK):
+                other = re_sb[t][:].indirect(half_sb[:, j0 // LIST_ROWS : (j0 + w) // LIST_ROWS])
+                if n in VECTOR_GATHERS:
+                    nc.vector.tensor_copy(ah[:, t, :], other)
+                else:
+                    nc.scalar.activation(ah[:, t, :], other, ACT.Copy)
+            rb = ring.tile([P, PACK * w], F32)
+            nc.vector.tensor_tensor(
+                rb[:].rearrange("p (b t j) -> p t b j", t=PACK, j=P),
+                ah[:].rearrange("p t (b j) -> p t b j", j=P),
+                c_sb[:, :, cols].rearrange("p t (b j) -> p t b j", j=P),
+                ALU.mult,
+            )
+            xc = ring.tile([P, PACK * w], F32)
+            nc.vector.tensor_tensor(xc[:], ra, rb[:], ALU.mult)
+            pa = ring.tile([P, D, w], F32)
+            pb = ring.tile([P, D, w], F32)
+            for sq, src in ((pa, ra), (pb, rb[:])):
+                nc.scalar.activation(
+                    sq[:].rearrange("p d (g i) -> p g d i", i=2),
+                    src.rearrange("p (g i d) -> p g d i", i=2, d=D),
+                    ACT.Square,
+                )
+
+            sab = bank("sab", 2)
+            nw = bank("nw", 2)
+            for k, sq in enumerate((pa, pb)):
+                for b in range(nb):
+                    for d in range(D):
+                        nc.tensor.matmul(
+                            sab[:, k * w + b * P : k * w + (b + 1) * P], sq[:, d, b * P : (b + 1) * P], ident[:],
+                            start=(d == 0), stop=(d == D - 1), is_transpose=True,
+                        )
+            for b in range(nb):
+                for d in range(D):
+                    nc.tensor.matmul(
+                        nw[:, b * P : (b + 1) * P], xc[:, b * P * D + d : (b + 1) * P * D : D], ident[:],
+                        start=(d == 0), stop=(d == D - 1), is_transpose=True,
+                    )
+
+            s_sb = ring.tile([P, PACK, w], F32)
+            per_bank = BANK // w
+            for t0 in range(0, PACK, per_bank):
+                im = bank("im", 3)
+                for t in range(t0, t0 + per_bank):
+                    product(im[:, (t - t0) * w : (t - t0 + 1) * w], w2w, w2s, t, cols)
+                nc.vector.scalar_tensor_tensor(
+                    s_sb[:, t0 : t0 + per_bank, :].rearrange("p t j -> p (t j)"), im[:], -0.4,
+                    ah[:, t0 : t0 + per_bank, :].rearrange("p t j -> p (t j)"), ALU.mult, ALU.add,
+                )
+
+            rs = ring.tile([P, 2 * w], F32)
+            nc.scalar.activation(rs[:], sab[:, 0 : 2 * w], ACT.Abs_reciprocal_sqrt, bias=0.3)
+            f1 = ring.tile([P, w], F32)
+            nc.vector.tensor_tensor(f1[:], nw[:, 0:w], rs[:, 0:w], ALU.mult)
+            fsc = ring.tile([P, w], F32)
+            nc.vector.tensor_tensor(fsc[:], f1[:], rs[:, w : 2 * w], ALU.mult)
+            mag = ring.tile([P, w], F32)
+            nc.scalar.activation(mag[:], fsc[:], ACT.Abs)
+            den2 = ring.tile([P, w], F32)
+            nc.scalar.activation(den2[:], mag[:], ACT.Square, bias=0.5)
+            inv = ring.tile([P, w], F32)
+            nc.scalar.activation(inv[:], den2[:], ACT.Abs_reciprocal_sqrt)
+            wien_t = ring.tile([P, w], F32)
+            nc.vector.scalar_tensor_tensor(wien_t[:], fsc[:], 0.6, inv[:], ALU.add, ALU.mult)
+            for b in range(nb):
+                nc.tensor.transpose(nw[:, w + b * P : w + (b + 1) * P], wien_t[:, b * P : (b + 1) * P], ident[:])
+
+            q = ring.tile([P, PACK * w], F32)
+            nc.vector.scalar_tensor_tensor(
+                q[:].rearrange("p (g d) -> p g d", d=D), nw[:, w : 2 * w].unsqueeze(2).to_broadcast([P, w, D]), 0.0,
+                ra.rearrange("p (g d) -> p g d", d=D), ALU.max, ALU.mult,
+            )
+            z = ring.tile([P, PACK, w], F32)
+            nc.vector.tensor_tensor(
+                z[:].rearrange("p t (b j) -> p t b j", j=P),
+                q[:].rearrange("p (b t j) -> p t b j", t=PACK, j=P),
+                s_sb[:].rearrange("p t (b j) -> p t b j", j=P),
+                ALU.add,
+            )
+            hid = ring.tile([P, w * PACK], BF16, align_bytes=64)
+            nc.vector.tensor_tensor(
+                hid[:].rearrange("p (c i t) -> p c t i", i=2, t=PACK),
+                z[:].rearrange("p t (c i) -> p c t i", i=2),
+                cu[:, :, cols].rearrange("p t (c i) -> p c t i", i=2),
+                ALU.mult,
+            )
+            codes = ring.tile([P, w], U32, align_bytes=64)
+            plane = ring.tile([P, w], U8, align_bytes=64)
+            nc.vector.quantize_mx(out=codes[:].bitcast(FP8X4), scales=plane[:], in_=hid[:])
+            o_ps = bank("o", 1)
+            nc.tensor.matmul_mx(
+                out=o_ps[:, 0:w], lhsT=w3w[:].bitcast(FP4X4), lhsT_scale=w3s,
+                rhs=codes[:].bitcast(FP8X4), rhs_scale=plane[:], start=True, stop=True,
+            )
+            o_sb = ring.tile([P, w], F32)
+            nc.scalar.copy(o_sb[:], o_ps[:, 0:w])
+            nc.sync.dma_start(out[:, cols], o_sb[:])
+            j0 = j0 + w

@@ -21,8 +21,13 @@ P = 128
 PACK = 4
 BANK = 512
 LIST_ROWS = 16
-CHUNKS = (128, 128, 256, 256, 128, 128)
-VECTOR_GATHERS = (1,)
+VECTOR_COPIES = ()
+RA_AT = 1
+VECTOR_SQUARES = 0
+VECTOR_SQB = 0
+VECTOR_FETCHES = ()
+AH_BUFS = 4
+SQ_BUFS = 1
 
 
 def tile_picked_ycryoem_ctf_p_kernel(
@@ -32,15 +37,15 @@ def tile_picked_ycryoem_ctf_p_kernel(
     with ExitStack() as ctx:
         lists = ctx.enter_context(tc.tile_pool(name="lists", bufs=1))
         keep = ctx.enter_context(tc.tile_pool(name="keep", bufs=1))
-        ring = ctx.enter_context(tc.tile_pool(name="ring", bufs=3))
+        ring = ctx.enter_context(tc.tile_pool(name="ring", bufs=4))
         psum = ctx.enter_context(tc.psum_pool(name="psum", bufs=1))
 
         def bank(tag, bufs):
             return psum.tile([P, BANK], F32, name=tag, tag=tag, bufs=bufs)
 
-        def load_scale_rows(queue, plane, scales):
+        def load_scale_rows(plane, scales):
             for q in range(4):
-                queue.dma_start(plane[32 * q : 32 * q + 4, :].bitcast(I32), scales[0, 4 * q : 4 * q + 4, :].bitcast(I32))
+                nc.sync.dma_start(plane[32 * q : 32 * q + 4, :].bitcast(I32), scales[0, 4 * q : 4 * q + 4, :].bitcast(I32))
 
         def deal(engine, dealt, raw, width):
             run = 16 // width
@@ -52,22 +57,22 @@ def tile_picked_ycryoem_ctf_p_kernel(
         offs_sb = lists.tile([P, S // LIST_ROWS], U16)
         half_sb = lists.tile([P, S // LIST_ROWS], U16)
         xw = keep.tile([P, T], I32, tag="first", bufs=1, align_bytes=64)
-        xs = keep.tile([P, T], U8, tag="second", bufs=1)
         w1_raw = keep.tile([P, 2 * H], U8, tag="third", bufs=1)
         ws_raw = keep.tile([P, H], U8, align_bytes=64)
-        u_sb = keep.tile([P, PACK], F32)
+        xs = keep.tile([P, T], U8, tag="second", bufs=1)
         ident = keep.tile([P, P], F32)
 
         nc.gpsimd.memset(xs[:].bitcast(I32), 0)
         nc.gpsimd.memset(ws_raw[:].bitcast(I32), 0)
         nc.sync.dma_start(offs_sb[:], offs)
+        nc.sync.dma_start(half_sb[:], half)
         nc.sync.dma_start(w1_raw[:].bitcast(I32), w1_words[0].bitcast(I32))
         nc.sync.dma_start(xw[:], x_words[0].rearrange("p n t -> p (n t)").bitcast(I32))
-        nc.sync.dma_start(half_sb[:], half)
-        load_scale_rows(nc.scalar, xs, x_scales)
-        load_scale_rows(nc.gpsimd, ws_raw, w1_scales)
-        nc.gpsimd.dma_start(u_sb[:], unit.rearrange("(p t) o -> p (t o)", t=PACK))
+        load_scale_rows(xs, x_scales)
+        load_scale_rows(ws_raw, w1_scales)
         make_identity(nc, ident[:])
+        warm = keep.tile([P, 1], F32)
+        nc.scalar.activation(warm[:], ident[:, 0:1], ACT.Abs_reciprocal_sqrt, bias=0.3)
 
         w1w = keep.tile([P, 2 * H], U8, align_bytes=64)
         w1s = keep.tile([P, H], U8, align_bytes=64)
@@ -76,48 +81,57 @@ def tile_picked_ycryoem_ctf_p_kernel(
         deal(nc.vector, w1w[:], w1_raw[:], 2)
         deal(nc.vector, w1s[:], ws_raw[:], 1)
 
-        c_sb = keep.tile([P, PACK, S], F32, tag="third", bufs=1)
+        cu_in = keep.tile([P, PACK * S + PACK], F32, tag="third", bufs=1)
+        c_sb = cu_in[:, 0 : PACK * S].rearrange("p (t j) -> p t j", t=PACK)
+        u_sb = cu_in[:, PACK * S : PACK * S + PACK]
         ctf_rows = ctf.rearrange("(p t) j -> p t j", t=PACK)
         for h in range(S // BANK):
-            for t0 in range(0, PACK, 2):
-                cols = slice(h * BANK, (h + 1) * BANK)
-                nc.sync.dma_start(c_sb[:, t0 : t0 + 2, cols], ctf_rows[:, t0 : t0 + 2, cols])
-        load_scale_rows(nc.sync, ws_raw, w2_scales)
+            cols = slice(h * BANK, (h + 1) * BANK)
+            nc.scalar.dma_start(c_sb[:, :, cols], ctf_rows[:, :, cols])
+        nc.scalar.dma_start(u_sb, unit.rearrange("(p t) o -> p (t o)", t=PACK))
+        load_scale_rows(ws_raw, w2_scales)
         deal(nc.gpsimd, w2s[:], ws_raw[:], 1)
 
-        gw = keep.tile([P, S], U32, align_bytes=64)
-        gs = keep.tile([P, S], U8, align_bytes=64)
+        halves = S // BANK
+        gw = [keep.tile([P, BANK], U32, name="gw%d" % h, align_bytes=64) for h in range(halves)]
+        gs = [keep.tile([P, BANK], U8, name="gs%d" % h, align_bytes=64) for h in range(halves)]
 
-        def product(dst, words, scales, t, cols):
+        def product(dst, words, scales, t, j0, width):
+            h, cols = j0 // BANK, slice(j0 % BANK, j0 % BANK + width)
             nc.tensor.matmul_mx(
                 out=dst,
                 lhsT=words[:, 2 * P * t : 2 * P * (t + 1)].bitcast(FP4X4),
                 lhsT_scale=scales[:, P * t : P * (t + 1)],
-                rhs=gw[:, cols].bitcast(FP8X4),
-                rhs_scale=gs[:, cols],
+                rhs=gw[h][:, cols].bitcast(FP8X4),
+                rhs_scale=gs[h][:, cols],
                 start=True,
                 stop=True,
             )
 
-        halves = S // BANK
-        nc.vector.tensor_copy(gs[:], xs[:].indirect(offs_sb[:]))
         re_sb = [keep.tile([P, S], F32, name="re%d" % t) for t in range(PACK)]
         ra_sb = [keep.tile([P, BANK // P, PACK, P], F32, name="ra%d" % h) for h in range(halves)]
-        re_banks = [("im", 3), ("im", 3), ("im", 3), ("o", 1), ("sab", 2), ("sab", 2), ("nw", 2), ("nw", 2)]
+        re_banks = [("sums", 5), ("sums", 5), ("im", 2), ("sums", 5), ("im", 2), ("sums", 5), ("sums", 5), ("o", 1)]
         for h in range(halves):
-            cols = slice(h * BANK, (h + 1) * BANK)
             picks = offs_sb[:, h * BANK // LIST_ROWS : (h + 1) * BANK // LIST_ROWS]
-            nc.vector.tensor_copy(gw[:, cols], xw[:].bitcast(U32).indirect(picks))
+            nc.vector.tensor_copy(gs[h][:], xs[:].indirect(picks))
+            nc.vector.tensor_copy(gw[h][:], xw[:].bitcast(U32).indirect(picks))
+        re_ps = {}
         for h in range(halves):
             cols = slice(h * BANK, (h + 1) * BANK)
             for t in range(PACK):
-                re_ps = bank(*re_banks[PACK * h + t])
-                product(re_ps[:], w1w, w1s, t, cols)
-                nc.scalar.copy(re_sb[t][:, cols], re_ps[:])
+                re_ps[h, t] = bank(*re_banks[PACK * h + t])
+                product(re_ps[h, t][:], w1w, w1s, t, h * BANK, BANK)
+                if PACK * h + t in VECTOR_COPIES:
+                    nc.vector.tensor_copy(re_sb[t][:, cols], re_ps[h, t][:])
+                else:
+                    nc.scalar.copy(re_sb[t][:, cols], re_ps[h, t][:])
+
+        def first_half_set(h):
+            for t in range(PACK):
                 nc.vector.tensor_tensor(
                     ra_sb[h][:, :, t, :],
-                    re_ps[:].rearrange("p (b j) -> p b j", j=P),
-                    c_sb[:, t, cols].rearrange("p (b j) -> p b j", j=P),
+                    re_ps[h, t][:].rearrange("p (b j) -> p b j", j=P),
+                    c_sb[:, t, h * BANK : (h + 1) * BANK].rearrange("p (b j) -> p b j", j=P),
                     ALU.mult,
                 )
 
@@ -127,116 +141,131 @@ def tile_picked_ycryoem_ctf_p_kernel(
         w3w = keep.tile([P, 2 * N], U8, tag="first", bufs=1, align_bytes=64)
         nc.sync.dma_start(w3w[:].bitcast(I32), w3_words[0].bitcast(I32))
         w3s = ws_raw[:, 0:N]
-        load_scale_rows(nc.sync, w3s, w3_scales)
+        load_scale_rows(w3s, w3_scales)
         cu = keep.tile([P, PACK, S], F32)
         for h in range(halves):
             cols = slice(h * BANK, (h + 1) * BANK)
             for t in range(PACK):
                 nc.gpsimd.tensor_scalar(cu[:, t, cols], c_sb[:, t, cols], u_sb[:, t : t + 1], 0.0, ALU.mult, ALU.add)
 
-        j0 = 0
-        for n, w in enumerate(CHUNKS):
-            cols = slice(j0, j0 + w)
-            nb = w // P
-            b0 = (j0 % BANK) // P
-            ra = ra_sb[j0 // BANK][:, b0 : b0 + nb, :, :].rearrange("p b t j -> p (b t j)")
-            ah = ring.tile([P, PACK, w], F32)
+        tiles = {}
+
+        def block_cols(n):
+            return slice(n * P, (n + 1) * P)
+
+        def ra_of(n):
+            return ra_sb[n * P // BANK][:, n % (BANK // P), :, :].rearrange("p t j -> p (t j)")
+
+        def fetch(n):
+            ah = tiles["ah", n] = ring.tile([P, PACK, P], F32, name="ah", bufs=AH_BUFS)
             for t in range(PACK):
-                other = re_sb[t][:].indirect(half_sb[:, j0 // LIST_ROWS : (j0 + w) // LIST_ROWS])
-                if n in VECTOR_GATHERS:
+                other = re_sb[t][:].indirect(half_sb[:, n * P // LIST_ROWS : (n + 1) * P // LIST_ROWS])
+                if n in VECTOR_FETCHES:
                     nc.vector.tensor_copy(ah[:, t, :], other)
                 else:
                     nc.scalar.activation(ah[:, t, :], other, ACT.Copy)
-            rb = ring.tile([P, PACK * w], F32)
+
+        def square(name, src, on_vector):
+            sq = ring.tile([P, D, P], F32, name=name, bufs=SQ_BUFS)
+            by_member = sq[:].rearrange("p d (g i) -> p g d i", i=2)
+            values = src.rearrange("p (g i d) -> p g d i", i=2, d=D)
+            if on_vector:
+                nc.vector.tensor_tensor(by_member, values, values, ALU.mult)
+            else:
+                nc.scalar.activation(by_member, values, ACT.Square)
+            return sq
+
+        def shell_sum(dst, term):
+            for d in range(D):
+                nc.tensor.matmul(dst, term(d), ident[:], start=(d == 0), stop=(d == D - 1), is_transpose=True)
+
+        def second_half_set(n):
+            rb = tiles["rb", n] = ring.tile([P, PACK * P], F32, name="rb")
             nc.vector.tensor_tensor(
-                rb[:].rearrange("p (b t j) -> p t b j", t=PACK, j=P),
-                ah[:].rearrange("p t (b j) -> p t b j", j=P),
-                c_sb[:, :, cols].rearrange("p t (b j) -> p t b j", j=P),
-                ALU.mult,
+                rb[:].rearrange("p (t j) -> p t j", t=PACK), tiles["ah", n][:], c_sb[:, :, block_cols(n)], ALU.mult
             )
-            xc = ring.tile([P, PACK * w], F32)
-            nc.vector.tensor_tensor(xc[:], ra, rb[:], ALU.mult)
-            pa = ring.tile([P, D, w], F32)
-            pb = ring.tile([P, D, w], F32)
-            for sq, src in ((pa, ra), (pb, rb[:])):
-                nc.scalar.activation(
-                    sq[:].rearrange("p d (g i) -> p g d i", i=2),
-                    src.rearrange("p (g i d) -> p g d i", i=2, d=D),
-                    ACT.Square,
-                )
+            pa = square("pa", ra_of(n), n < VECTOR_SQUARES)
+            pb = square("pb", rb[:], n < VECTOR_SQB)
+            sums = tiles["sums", n] = bank("sums", 5)
+            shell_sum(sums[:, 0:P], lambda d: pa[:, d, :])
+            shell_sum(sums[:, P : 2 * P], lambda d: pb[:, d, :])
 
-            sab = bank("sab", 2)
-            nw = bank("nw", 2)
-            for k, sq in enumerate((pa, pb)):
-                for b in range(nb):
-                    for d in range(D):
-                        nc.tensor.matmul(
-                            sab[:, k * w + b * P : k * w + (b + 1) * P], sq[:, d, b * P : (b + 1) * P], ident[:],
-                            start=(d == 0), stop=(d == D - 1), is_transpose=True,
-                        )
-            for b in range(nb):
-                for d in range(D):
-                    nc.tensor.matmul(
-                        nw[:, b * P : (b + 1) * P], xc[:, b * P * D + d : (b + 1) * P * D : D], ident[:],
-                        start=(d == 0), stop=(d == D - 1), is_transpose=True,
-                    )
+        def cross(n):
+            xc = ring.tile([P, PACK * P], F32)
+            nc.vector.tensor_tensor(xc[:], ra_of(n), tiles["rb", n][:], ALU.mult)
+            shell_sum(tiles["sums", n][:, 2 * P : 3 * P], lambda d: xc[:, d : PACK * P : D])
 
-            s_sb = ring.tile([P, PACK, w], F32)
-            per_bank = BANK // w
-            for t0 in range(0, PACK, per_bank):
-                im = bank("im", 3)
-                for t in range(t0, t0 + per_bank):
-                    product(im[:, (t - t0) * w : (t - t0 + 1) * w], w2w, w2s, t, cols)
-                nc.vector.scalar_tensor_tensor(
-                    s_sb[:, t0 : t0 + per_bank, :].rearrange("p t j -> p (t j)"), im[:], -0.4,
-                    ah[:, t0 : t0 + per_bank, :].rearrange("p t j -> p (t j)"), ALU.mult, ALU.add,
-                )
-
-            rs = ring.tile([P, 2 * w], F32)
-            nc.scalar.activation(rs[:], sab[:, 0 : 2 * w], ACT.Abs_reciprocal_sqrt, bias=0.3)
-            f1 = ring.tile([P, w], F32)
-            nc.vector.tensor_tensor(f1[:], nw[:, 0:w], rs[:, 0:w], ALU.mult)
-            fsc = ring.tile([P, w], F32)
-            nc.vector.tensor_tensor(fsc[:], f1[:], rs[:, w : 2 * w], ALU.mult)
-            mag = ring.tile([P, w], F32)
-            nc.scalar.activation(mag[:], fsc[:], ACT.Abs)
-            den2 = ring.tile([P, w], F32)
-            nc.scalar.activation(den2[:], mag[:], ACT.Square, bias=0.5)
-            inv = ring.tile([P, w], F32)
-            nc.scalar.activation(inv[:], den2[:], ACT.Abs_reciprocal_sqrt)
-            wien_t = ring.tile([P, w], F32)
-            nc.vector.scalar_tensor_tensor(wien_t[:], fsc[:], 0.6, inv[:], ALU.add, ALU.mult)
-            for b in range(nb):
-                nc.tensor.transpose(nw[:, w + b * P : w + (b + 1) * P], wien_t[:, b * P : (b + 1) * P], ident[:])
-
-            q = ring.tile([P, PACK * w], F32)
+        def rest(n):
+            im = bank("im", 2)
+            for t in range(PACK):
+                product(im[:, t * P : (t + 1) * P], w2w, w2s, t, n * P, P)
+            s_sb = tiles["s", n] = ring.tile([P, PACK * P], F32, name="s_sb")
             nc.vector.scalar_tensor_tensor(
-                q[:].rearrange("p (g d) -> p g d", d=D), nw[:, w : 2 * w].unsqueeze(2).to_broadcast([P, w, D]), 0.0,
-                ra.rearrange("p (g d) -> p g d", d=D), ALU.max, ALU.mult,
+                s_sb[:], im[:], -0.4, tiles["ah", n][:].rearrange("p t j -> p (t j)"), ALU.mult, ALU.add
             )
-            z = ring.tile([P, PACK, w], F32)
-            nc.vector.tensor_tensor(
-                z[:].rearrange("p t (b j) -> p t b j", j=P),
-                q[:].rearrange("p (b t j) -> p t b j", t=PACK, j=P),
-                s_sb[:].rearrange("p t (b j) -> p t b j", j=P),
-                ALU.add,
+
+        def norm_a(n):
+            sums = tiles["sums", n]
+            rs = tiles["rs", n] = ring.tile([P, 2 * P], F32, name="rs")
+            nc.scalar.activation(rs[:], sums[:, 0 : 2 * P], ACT.Abs_reciprocal_sqrt, bias=0.3)
+            f1 = tiles["f1", n] = ring.tile([P, P], F32, name="f1")
+            nc.vector.tensor_tensor(f1[:], sums[:, 2 * P : 3 * P], rs[:, 0:P], ALU.mult)
+
+        def norm_b(n):
+            fsc = tiles["fsc", n] = ring.tile([P, P], F32, name="fsc")
+            nc.vector.tensor_tensor(fsc[:], tiles["f1", n][:], tiles["rs", n][:, P : 2 * P], ALU.mult)
+            mag = ring.tile([P, P], F32)
+            nc.scalar.activation(mag[:], fsc[:], ACT.Abs)
+            den2 = ring.tile([P, P], F32)
+            nc.scalar.activation(den2[:], mag[:], ACT.Square, bias=0.5)
+            inv = tiles["inv", n] = ring.tile([P, P], F32, name="inv")
+            nc.scalar.activation(inv[:], den2[:], ACT.Abs_reciprocal_sqrt)
+
+        def weight(n):
+            wien_t = ring.tile([P, P], F32)
+            nc.vector.scalar_tensor_tensor(wien_t[:], tiles["fsc", n][:], 0.6, tiles["inv", n][:], ALU.add, ALU.mult)
+            nc.tensor.transpose(tiles["sums", n][:, 3 * P : 4 * P], wien_t[:], ident[:])
+
+        def filtered(n):
+            q = tiles["q", n] = ring.tile([P, PACK * P], F32, name="q")
+            nc.vector.scalar_tensor_tensor(
+                q[:].rearrange("p (g d) -> p g d", d=D),
+                tiles["sums", n][:, 3 * P : 4 * P].unsqueeze(2).to_broadcast([P, P, D]), 0.0,
+                ra_of(n).rearrange("p (g d) -> p g d", d=D), ALU.max, ALU.mult,
             )
-            hid = ring.tile([P, w * PACK], BF16, align_bytes=64)
+
+        def joined(n):
+            z = tiles["z", n] = ring.tile([P, PACK * P], F32, name="z")
+            nc.vector.tensor_tensor(z[:], tiles["q", n][:], tiles["s", n][:], ALU.add)
+
+        def hidden(n):
+            hid = tiles["hid", n] = ring.tile([P, P * PACK], BF16, name="hid", align_bytes=64)
             nc.vector.tensor_tensor(
                 hid[:].rearrange("p (c i t) -> p c t i", i=2, t=PACK),
-                z[:].rearrange("p t (c i) -> p c t i", i=2),
-                cu[:, :, cols].rearrange("p t (c i) -> p c t i", i=2),
+                tiles["z", n][:].rearrange("p (t c i) -> p c t i", i=2, t=PACK),
+                cu[:, :, block_cols(n)].rearrange("p t (c i) -> p c t i", i=2),
                 ALU.mult,
             )
-            codes = ring.tile([P, w], U32, align_bytes=64)
-            plane = ring.tile([P, w], U8, align_bytes=64)
-            nc.vector.quantize_mx(out=codes[:].bitcast(FP8X4), scales=plane[:], in_=hid[:])
+
+        def voxels(n):
+            codes = ring.tile([P, P], U32, align_bytes=64)
+            plane = ring.tile([P, P], U8, align_bytes=64)
+            nc.vector.quantize_mx(out=codes[:].bitcast(FP8X4), scales=plane[:], in_=tiles["hid", n][:])
             o_ps = bank("o", 1)
             nc.tensor.matmul_mx(
-                out=o_ps[:, 0:w], lhsT=w3w[:].bitcast(FP4X4), lhsT_scale=w3s,
+                out=o_ps[:, 0:P], lhsT=w3w[:].bitcast(FP4X4), lhsT_scale=w3s,
                 rhs=codes[:].bitcast(FP8X4), rhs_scale=plane[:], start=True, stop=True,
             )
-            o_sb = ring.tile([P, w], F32)
-            nc.scalar.copy(o_sb[:], o_ps[:, 0:w])
-            nc.sync.dma_start(out[:, cols], o_sb[:])
-            j0 = j0 + w
+            o_sb = ring.tile([P, P], F32)
+            nc.scalar.copy(o_sb[:], o_ps[:, 0:P])
+            nc.sync.dma_start(out[:, block_cols(n)], o_sb[:])
+
+        stages = [(second_half_set,1),(weight,4),(cross,1),(norm_b,3),(fetch,0),(hidden,5),(norm_a,2),(filtered,4),(voxels,5),(rest,2),(joined,4)]
+        blocks = S // P
+        first_half_set(0)
+        for step in range(blocks + max(lag for stage, lag in stages)):
+            if step == RA_AT:
+                first_half_set(1)
+            for stage, lag in stages:
+                if 0 <= step - lag < blocks:
+                    stage(step - lag)

@@ -23,9 +23,9 @@ BANK = 512
 LIST_ROWS = 16
 VECTOR_COPIES = ()
 RA_AT = 1
-VECTOR_SQUARES = 0
+VECTOR_SQUARES = 2
 VECTOR_SQB = 0
-VECTOR_FETCHES = ()
+VECTOR_FETCHES = (1,)
 AH_BUFS = 4
 SQ_BUFS = 1
 
@@ -36,6 +36,7 @@ def tile_picked_ycryoem_ctf_p_kernel(
     nc = tc.nc
     with ExitStack() as ctx:
         lists = ctx.enter_context(tc.tile_pool(name="lists", bufs=1))
+        picked = ctx.enter_context(tc.tile_pool(name="picked", bufs=1))
         keep = ctx.enter_context(tc.tile_pool(name="keep", bufs=1))
         ring = ctx.enter_context(tc.tile_pool(name="ring", bufs=4))
         psum = ctx.enter_context(tc.psum_pool(name="psum", bufs=1))
@@ -43,9 +44,9 @@ def tile_picked_ycryoem_ctf_p_kernel(
         def bank(tag, bufs):
             return psum.tile([P, BANK], F32, name=tag, tag=tag, bufs=bufs)
 
-        def load_scale_rows(plane, scales):
-            for q in range(4):
-                nc.sync.dma_start(plane[32 * q : 32 * q + 4, :].bitcast(I32), scales[0, 4 * q : 4 * q + 4, :].bitcast(I32))
+        def load_scale_rows(plane, scales, last=nc.sync):
+            for q, queue in enumerate((nc.sync, nc.sync, nc.sync, last)):
+                queue.dma_start(plane[32 * q : 32 * q + 4, :].bitcast(I32), scales[0, 4 * q : 4 * q + 4, :].bitcast(I32))
 
         def deal(engine, dealt, raw, width):
             run = 16 // width
@@ -59,42 +60,54 @@ def tile_picked_ycryoem_ctf_p_kernel(
         xw = keep.tile([P, T], I32, tag="first", bufs=1, align_bytes=64)
         w1_raw = keep.tile([P, 2 * H], U8, tag="third", bufs=1)
         ws_raw = keep.tile([P, H], U8, align_bytes=64)
-        xs = keep.tile([P, T], U8, tag="second", bufs=1)
+        w1s_raw = picked.tile([P, H], U8, offset=BANK // 2)
+        xs = keep.tile([P, T], U8)
         ident = keep.tile([P, P], F32)
 
+        warm = keep.tile([P, 2], F32)
+        nc.vector.memset(warm[:, 0:1], 1.0)
+        nc.scalar.activation(warm[:, 1:2], warm[:, 0:1], ACT.Abs_reciprocal_sqrt)
         nc.gpsimd.memset(xs[:].bitcast(I32), 0)
-        nc.gpsimd.memset(ws_raw[:].bitcast(I32), 0)
+        nc.gpsimd.memset(w1s_raw[:].bitcast(I32), 0)
         nc.sync.dma_start(offs_sb[:], offs)
         nc.sync.dma_start(half_sb[:], half)
         nc.sync.dma_start(w1_raw[:].bitcast(I32), w1_words[0].bitcast(I32))
         nc.sync.dma_start(xw[:], x_words[0].rearrange("p n t -> p (n t)").bitcast(I32))
         load_scale_rows(xs, x_scales)
-        load_scale_rows(ws_raw, w1_scales)
+        load_scale_rows(w1s_raw, w1_scales, nc.gpsimd)
+        nc.gpsimd.memset(ws_raw[:].bitcast(I32), 0)
+        w2_raw = keep.tile([P, 2 * H], U8)
+        nc.gpsimd.dma_start(w2_raw[:].bitcast(I32), w2_words[0].bitcast(I32))
         make_identity(nc, ident[:])
-        warm = keep.tile([P, 1], F32)
-        nc.scalar.activation(warm[:], ident[:, 0:1], ACT.Abs_reciprocal_sqrt, bias=0.3)
 
         w1w = keep.tile([P, 2 * H], U8, align_bytes=64)
         w1s = keep.tile([P, H], U8, align_bytes=64)
         w2w = keep.tile([P, 2 * H], U8, align_bytes=64)
         w2s = keep.tile([P, H], U8, align_bytes=64)
         deal(nc.vector, w1w[:], w1_raw[:], 2)
-        deal(nc.vector, w1s[:], ws_raw[:], 1)
+        deal(nc.vector, w1s[:], w1s_raw[:], 1)
 
         cu_in = keep.tile([P, PACK * S + PACK], F32, tag="third", bufs=1)
         c_sb = cu_in[:, 0 : PACK * S].rearrange("p (t j) -> p t j", t=PACK)
         u_sb = cu_in[:, PACK * S : PACK * S + PACK]
+        nc.scalar.dma_start(u_sb, unit.rearrange("(p t) o -> p (t o)", t=PACK))
         ctf_rows = ctf.rearrange("(p t) j -> p t j", t=PACK)
         for h in range(S // BANK):
             cols = slice(h * BANK, (h + 1) * BANK)
             nc.scalar.dma_start(c_sb[:, :, cols], ctf_rows[:, :, cols])
-        nc.scalar.dma_start(u_sb, unit.rearrange("(p t) o -> p (t o)", t=PACK))
+        deal(nc.gpsimd, w2w[:], w2_raw[:], 2)
         load_scale_rows(ws_raw, w2_scales)
         deal(nc.gpsimd, w2s[:], ws_raw[:], 1)
 
         halves = S // BANK
-        gw = [keep.tile([P, BANK], U32, name="gw%d" % h, align_bytes=64) for h in range(halves)]
-        gs = [keep.tile([P, BANK], U8, name="gs%d" % h, align_bytes=64) for h in range(halves)]
+        gw = [
+            keep.tile([P, BANK], U32, name="gw0", align_bytes=64),
+            picked.tile([P, BANK], U32, name="gw1", align_bytes=64, offset=BANK),
+        ]
+        gs = [
+            keep.tile([P, BANK], U8, name="gs0", align_bytes=64),
+            picked.tile([P, BANK], U8, name="gs1", align_bytes=64, offset=0),
+        ]
 
         def product(dst, words, scales, t, j0, width):
             h, cols = j0 // BANK, slice(j0 % BANK, j0 % BANK + width)
@@ -135,9 +148,6 @@ def tile_picked_ycryoem_ctf_p_kernel(
                     ALU.mult,
                 )
 
-        w2_raw = keep.tile([P, 2 * H], U8, tag="second", bufs=1)
-        nc.sync.dma_start(w2_raw[:].bitcast(I32), w2_words[0].bitcast(I32))
-        deal(nc.gpsimd, w2w[:], w2_raw[:], 2)
         w3w = keep.tile([P, 2 * N], U8, tag="first", bufs=1, align_bytes=64)
         nc.sync.dma_start(w3w[:].bitcast(I32), w3_words[0].bitcast(I32))
         w3s = ws_raw[:, 0:N]
@@ -192,7 +202,7 @@ def tile_picked_ycryoem_ctf_p_kernel(
 
         def cross(n):
             xc = ring.tile([P, PACK * P], F32)
-            nc.vector.tensor_tensor(xc[:], ra_of(n), tiles["rb", n][:], ALU.mult)
+            (nc.gpsimd if n >= 2 else nc.vector).tensor_tensor(xc[:], ra_of(n), tiles["rb", n][:], ALU.mult)
             shell_sum(tiles["sums", n][:, 2 * P : 3 * P], lambda d: xc[:, d : PACK * P : D])
 
         def rest(n):
@@ -241,9 +251,9 @@ def tile_picked_ycryoem_ctf_p_kernel(
         def hidden(n):
             hid = tiles["hid", n] = ring.tile([P, P * PACK], BF16, name="hid", align_bytes=64)
             nc.vector.tensor_tensor(
-                hid[:].rearrange("p (c i t) -> p c t i", i=2, t=PACK),
-                tiles["z", n][:].rearrange("p (t c i) -> p c t i", i=2, t=PACK),
-                cu[:, :, block_cols(n)].rearrange("p t (c i) -> p c t i", i=2),
+                hid[:].rearrange("p (c i t) -> p c t i", i=4, t=PACK),
+                tiles["z", n][:].rearrange("p (t c i) -> p c t i", i=4, t=PACK),
+                cu[:, :, block_cols(n)].rearrange("p t (c i) -> p c t i", i=4),
                 ALU.mult,
             )
 
@@ -260,7 +270,7 @@ def tile_picked_ycryoem_ctf_p_kernel(
             nc.scalar.copy(o_sb[:], o_ps[:, 0:P])
             nc.sync.dma_start(out[:, block_cols(n)], o_sb[:])
 
-        stages = [(second_half_set,1),(weight,4),(cross,1),(norm_b,3),(fetch,0),(hidden,5),(norm_a,2),(filtered,4),(voxels,5),(rest,2),(joined,4)]
+        stages = [(second_half_set,1),(cross,1),(filtered,5),(rest,1),(norm_a,3),(fetch,0),(weight,4),(hidden,6),(norm_b,3),(joined,5),(voxels,6)]
         blocks = S // P
         first_half_set(0)
         for step in range(blocks + max(lag for stage, lag in stages)):

from contextlib import ExitStack

import concourse.mybir as mybir
from concourse.masks import make_identity

K, T, S, D, N, H = 512, 2048, 1024, 4, 128, 512
FLOPS = 2 * K * H * S * 2 + 2 * H * N * S

F32 = mybir.dt.float32
BF16 = mybir.dt.bfloat16
I32 = mybir.dt.int32
U32 = mybir.dt.uint32
U16 = mybir.dt.uint16
U8 = mybir.dt.uint8
FP8X4 = mybir.dt.float8_e4m3fn_x4
FP4X4 = mybir.dt.float4_e2m1fn_x4
ACT = mybir.ActivationFunctionType
ALU = mybir.AluOpType

P = 128
PACK = 4
BANK = 512
LIST_ROWS = 16
VECTOR_COPIES = ()
RA_AT = 1
VECTOR_SQUARES = 2
VECTOR_SQB = 0
VECTOR_FETCHES = (1,)
AH_BUFS = 4
SQ_BUFS = 1


def tile_picked_ycryoem_ctf_p_kernel(
    tc, x_words, x_scales, w1_words, w1_scales, w2_words, w2_scales, ctf, unit, w3_words, w3_scales, offs, half, out
):
    nc = tc.nc
    with ExitStack() as ctx:
        lists = ctx.enter_context(tc.tile_pool(name="lists", bufs=1))
        picked = ctx.enter_context(tc.tile_pool(name="picked", bufs=1))
        keep = ctx.enter_context(tc.tile_pool(name="keep", bufs=1))
        ring = ctx.enter_context(tc.tile_pool(name="ring", bufs=4))
        psum = ctx.enter_context(tc.psum_pool(name="psum", bufs=1))

        def bank(tag, bufs):
            return psum.tile([P, BANK], F32, name=tag, tag=tag, bufs=bufs)

        def load_scale_rows(plane, scales, last=nc.sync):
            for q, queue in enumerate((nc.sync, nc.sync, nc.sync, last)):
                queue.dma_start(plane[32 * q : 32 * q + 4, :].bitcast(I32), scales[0, 4 * q : 4 * q + 4, :].bitcast(I32))

        def deal(engine, dealt, raw, width):
            run = 16 // width
            engine.tensor_copy(
                dealt.rearrange("p (t c i b) -> p c t i b", t=PACK, i=run, b=width),
                raw.rearrange("p (c i t b) -> p c t i b", t=PACK, i=run, b=width),
            )

        offs_sb = lists.tile([P, S // LIST_ROWS], U16)
        half_sb = lists.tile([P, S // LIST_ROWS], U16)
        xw = keep.tile([P, T], I32, tag="first", bufs=1, align_bytes=64)
        w1_raw = keep.tile([P, 2 * H], U8, tag="third", bufs=1)
        ws_raw = keep.tile([P, H], U8, align_bytes=64)
        w1s_raw = picked.tile([P, H], U8, offset=BANK // 2)
        xs = keep.tile([P, T], U8)
        ident = keep.tile([P, P], F32)

        warm = keep.tile([P, 2], F32)
        nc.vector.memset(warm[:, 0:1], 1.0)
        nc.scalar.activation(warm[:, 1:2], warm[:, 0:1], ACT.Abs_reciprocal_sqrt)
        nc.gpsimd.memset(xs[:].bitcast(I32), 0)
        nc.gpsimd.memset(w1s_raw[:].bitcast(I32), 0)
        nc.sync.dma_start(offs_sb[:], offs)
        nc.sync.dma_start(half_sb[:], half)
        nc.sync.dma_start(w1_raw[:].bitcast(I32), w1_words[0].bitcast(I32))
        nc.sync.dma_start(xw[:], x_words[0].rearrange("p n t -> p (n t)").bitcast(I32))
        load_scale_rows(xs, x_scales)
        load_scale_rows(w1s_raw, w1_scales, nc.gpsimd)
        nc.gpsimd.memset(ws_raw[:].bitcast(I32), 0)
        w2_raw = keep.tile([P, 2 * H], U8)
        nc.gpsimd.dma_start(w2_raw[:].bitcast(I32), w2_words[0].bitcast(I32))
        make_identity(nc, ident[:])

        w1w = keep.tile([P, 2 * H], U8, align_bytes=64)
        w1s = keep.tile([P, H], U8, align_bytes=64)
        w2w = keep.tile([P, 2 * H], U8, align_bytes=64)
        w2s = keep.tile([P, H], U8, align_bytes=64)
        deal(nc.vector, w1w[:], w1_raw[:], 2)
        deal(nc.vector, w1s[:], w1s_raw[:], 1)

        cu_in = keep.tile([P, PACK * S + PACK], F32, tag="third", bufs=1)
        c_sb = cu_in[:, 0 : PACK * S].rearrange("p (t j) -> p t j", t=PACK)
        u_sb = cu_in[:, PACK * S : PACK * S + PACK]
        nc.scalar.dma_start(u_sb, unit.rearrange("(p t) o -> p (t o)", t=PACK))
        ctf_rows = ctf.rearrange("(p t) j -> p t j", t=PACK)
        for h in range(S // BANK):
            cols = slice(h * BANK, (h + 1) * BANK)
            nc.scalar.dma_start(c_sb[:, :, cols], ctf_rows[:, :, cols])
        deal(nc.gpsimd, w2w[:], w2_raw[:], 2)
        load_scale_rows(ws_raw, w2_scales)
        deal(nc.gpsimd, w2s[:], ws_raw[:], 1)

        halves = S // BANK
        gw = [
            keep.tile([P, BANK], U32, name="gw0", align_bytes=64),
            picked.tile([P, BANK], U32, name="gw1", align_bytes=64, offset=BANK),
        ]
        gs = [
            keep.tile([P, BANK], U8, name="gs0", align_bytes=64),
            picked.tile([P, BANK], U8, name="gs1", align_bytes=64, offset=0),
        ]

        def product(dst, words, scales, t, j0, width):
            h, cols = j0 // BANK, slice(j0 % BANK, j0 % BANK + width)
            nc.tensor.matmul_mx(
                out=dst,
                lhsT=words[:, 2 * P * t : 2 * P * (t + 1)].bitcast(FP4X4),
                lhsT_scale=scales[:, P * t : P * (t + 1)],
                rhs=gw[h][:, cols].bitcast(FP8X4),
                rhs_scale=gs[h][:, cols],
                start=True,
                stop=True,
            )

        re_sb = [keep.tile([P, S], F32, name="re%d" % t) for t in range(PACK)]
        ra_sb = [keep.tile([P, BANK // P, PACK, P], F32, name="ra%d" % h) for h in range(halves)]
        re_banks = [("sums", 5), ("sums", 5), ("im", 2), ("sums", 5), ("im", 2), ("sums", 5), ("sums", 5), ("o", 1)]
        for h in range(halves):
            picks = offs_sb[:, h * BANK // LIST_ROWS : (h + 1) * BANK // LIST_ROWS]
            nc.vector.tensor_copy(gs[h][:], xs[:].indirect(picks))
            nc.vector.tensor_copy(gw[h][:], xw[:].bitcast(U32).indirect(picks))
        re_ps = {}
        for h in range(halves):
            cols = slice(h * BANK, (h + 1) * BANK)
            for t in range(PACK):
                re_ps[h, t] = bank(*re_banks[PACK * h + t])
                product(re_ps[h, t][:], w1w, w1s, t, h * BANK, BANK)
                if PACK * h + t in VECTOR_COPIES:
                    nc.vector.tensor_copy(re_sb[t][:, cols], re_ps[h, t][:])
                else:
                    nc.scalar.copy(re_sb[t][:, cols], re_ps[h, t][:])

        def first_half_set(h):
            for t in range(PACK):
                nc.vector.tensor_tensor(
                    ra_sb[h][:, :, t, :],
                    re_ps[h, t][:].rearrange("p (b j) -> p b j", j=P),
                    c_sb[:, t, h * BANK : (h + 1) * BANK].rearrange("p (b j) -> p b j", j=P),
                    ALU.mult,
                )

        w3w = keep.tile([P, 2 * N], U8, tag="first", bufs=1, align_bytes=64)
        nc.sync.dma_start(w3w[:].bitcast(I32), w3_words[0].bitcast(I32))
        w3s = ws_raw[:, 0:N]
        load_scale_rows(w3s, w3_scales)
        cu = keep.tile([P, PACK, S], F32)
        for h in range(halves):
            cols = slice(h * BANK, (h + 1) * BANK)
            for t in range(PACK):
                nc.gpsimd.tensor_scalar(cu[:, t, cols], c_sb[:, t, cols], u_sb[:, t : t + 1], 0.0, ALU.mult, ALU.add)

        tiles = {}

        def block_cols(n):
            return slice(n * P, (n + 1) * P)

        def ra_of(n):
            return ra_sb[n * P // BANK][:, n % (BANK // P), :, :].rearrange("p t j -> p (t j)")

        def fetch(n):
            ah = tiles["ah", n] = ring.tile([P, PACK, P], F32, name="ah", bufs=AH_BUFS)
            for t in range(PACK):
                other = re_sb[t][:].indirect(half_sb[:, n * P // LIST_ROWS : (n + 1) * P // LIST_ROWS])
                if n in VECTOR_FETCHES:
                    nc.vector.tensor_copy(ah[:, t, :], other)
                else:
                    nc.scalar.activation(ah[:, t, :], other, ACT.Copy)

        def square(name, src, on_vector):
            sq = ring.tile([P, D, P], F32, name=name, bufs=SQ_BUFS)
            by_member = sq[:].rearrange("p d (g i) -> p g d i", i=2)
            values = src.rearrange("p (g i d) -> p g d i", i=2, d=D)
            if on_vector:
                nc.vector.tensor_tensor(by_member, values, values, ALU.mult)
            else:
                nc.scalar.activation(by_member, values, ACT.Square)
            return sq

        def shell_sum(dst, term):
            for d in range(D):
                nc.tensor.matmul(dst, term(d), ident[:], start=(d == 0), stop=(d == D - 1), is_transpose=True)

        def second_half_set(n):
            rb = tiles["rb", n] = ring.tile([P, PACK * P], F32, name="rb")
            nc.vector.tensor_tensor(
                rb[:].rearrange("p (t j) -> p t j", t=PACK), tiles["ah", n][:], c_sb[:, :, block_cols(n)], ALU.mult
            )
            pa = square("pa", ra_of(n), n < VECTOR_SQUARES)
            pb = square("pb", rb[:], n < VECTOR_SQB)
            sums = tiles["sums", n] = bank("sums", 5)
            shell_sum(sums[:, 0:P], lambda d: pa[:, d, :])
            shell_sum(sums[:, P : 2 * P], lambda d: pb[:, d, :])

        def cross(n):
            xc = ring.tile([P, PACK * P], F32)
            (nc.gpsimd if n >= 2 else nc.vector).tensor_tensor(xc[:], ra_of(n), tiles["rb", n][:], ALU.mult)
            shell_sum(tiles["sums", n][:, 2 * P : 3 * P], lambda d: xc[:, d : PACK * P : D])

        def rest(n):
            im = bank("im", 2)
            for t in range(PACK):
                product(im[:, t * P : (t + 1) * P], w2w, w2s, t, n * P, P)
            s_sb = tiles["s", n] = ring.tile([P, PACK * P], F32, name="s_sb")
            nc.vector.scalar_tensor_tensor(
                s_sb[:], im[:], -0.4, tiles["ah", n][:].rearrange("p t j -> p (t j)"), ALU.mult, ALU.add
            )

        def norm_a(n):
            sums = tiles["sums", n]
            rs = tiles["rs", n] = ring.tile([P, 2 * P], F32, name="rs")
            nc.scalar.activation(rs[:], sums[:, 0 : 2 * P], ACT.Abs_reciprocal_sqrt, bias=0.3)
            f1 = tiles["f1", n] = ring.tile([P, P], F32, name="f1")
            nc.vector.tensor_tensor(f1[:], sums[:, 2 * P : 3 * P], rs[:, 0:P], ALU.mult)

        def norm_b(n):
            fsc = tiles["fsc", n] = ring.tile([P, P], F32, name="fsc")
            nc.vector.tensor_tensor(fsc[:], tiles["f1", n][:], tiles["rs", n][:, P : 2 * P], ALU.mult)
            mag = ring.tile([P, P], F32)
            nc.scalar.activation(mag[:], fsc[:], ACT.Abs)
            den2 = ring.tile([P, P], F32)
            nc.scalar.activation(den2[:], mag[:], ACT.Square, bias=0.5)
            inv = tiles["inv", n] = ring.tile([P, P], F32, name="inv")
            nc.scalar.activation(inv[:], den2[:], ACT.Abs_reciprocal_sqrt)

        def weight(n):
            wien_t = ring.tile([P, P], F32)
            nc.vector.scalar_tensor_tensor(wien_t[:], tiles["fsc", n][:], 0.6, tiles["inv", n][:], ALU.add, ALU.mult)
            nc.tensor.transpose(tiles["sums", n][:, 3 * P : 4 * P], wien_t[:], ident[:])

        def filtered(n):
            q = tiles["q", n] = ring.tile([P, PACK * P], F32, name="q")
            nc.vector.scalar_tensor_tensor(
                q[:].rearrange("p (g d) -> p g d", d=D),
                tiles["sums", n][:, 3 * P : 4 * P].unsqueeze(2).to_broadcast([P, P, D]), 0.0,
                ra_of(n).rearrange("p (g d) -> p g d", d=D), ALU.max, ALU.mult,
            )

        def joined(n):
            z = tiles["z", n] = ring.tile([P, PACK * P], F32, name="z")
            nc.vector.tensor_tensor(z[:], tiles["q", n][:], tiles["s", n][:], ALU.add)

        def hidden(n):
            hid = tiles["hid", n] = ring.tile([P, P * PACK], BF16, name="hid", align_bytes=64)
            nc.vector.tensor_tensor(
                hid[:].rearrange("p (c i t) -> p c t i", i=4, t=PACK),
                tiles["z", n][:].rearrange("p (t c i) -> p c t i", i=4, t=PACK),
                cu[:, :, block_cols(n)].rearrange("p t (c i) -> p c t i", i=4),
                ALU.mult,
            )

        def voxels(n):
            codes = ring.tile([P, P], U32, align_bytes=64)
            plane = ring.tile([P, P], U8, align_bytes=64)
            nc.vector.quantize_mx(out=codes[:].bitcast(FP8X4), scales=plane[:], in_=tiles["hid", n][:])
            o_ps = bank("o", 1)
            nc.tensor.matmul_mx(
                out=o_ps[:, 0:P], lhsT=w3w[:].bitcast(FP4X4), lhsT_scale=w3s,
                rhs=codes[:].bitcast(FP8X4), rhs_scale=plane[:], start=True, stop=True,
            )
            o_sb = ring.tile([P, P], F32)
            nc.scalar.copy(o_sb[:], o_ps[:, 0:P])
            nc.sync.dma_start(out[:, block_cols(n)], o_sb[:])

        stages = [(second_half_set,1),(cross,1),(filtered,5),(rest,1),(norm_a,3),(fetch,0),(weight,4),(hidden,6),(norm_b,3),(joined,5),(voxels,6)]
        blocks = S // P
        first_half_set(0)
        for step in range(blocks + max(lag for stage, lag in stages)):
            if step == RA_AT:
                first_half_set(1)
            for stage, lag in stages:
                if 0 <= step - lag < blocks:
                    stage(step - lag)
